import numpy as np, ml_dtypes
CORES = [7,391,135,263,15,399,143,271]
N = 8
C = 128
def setup_inputs(rng):
    x = rng.standard_normal((N, 128, C), dtype=np.float32) * (0.25 + np.abs(rng.standard_normal((N, 1, C), dtype=np.float32)))
    return {"x": x.astype(ml_dtypes.bfloat16)}
def setup_inputs_big(rng):
    d = setup_inputs(rng)
    for k in ("x",): d[k] = (d[k].astype(np.float32) * 1048576.0).astype(d[k].dtype)
    return d
def setup_inputs_small(rng):
    d = setup_inputs(rng)
    for k in ("x",): d[k] = (d[k].astype(np.float32) * (1 / 1048576.0)).astype(d[k].dtype)
    return d
def setup_inputs_apart(rng):
    d = setup_inputs(rng)
    f = (10.0 ** rng.permutation(np.linspace(-1.5, 1.5, N))).astype(np.float32).reshape(N, 1, 1)
    for k in ("x",): d[k] = (d[k].astype(np.float32) * f).astype(d[k].dtype)
    return d
def setup_inputs_mixed(rng):
    d = setup_inputs(rng)
    f = (10.0 ** rng.uniform(-3, 3, (N, 1, C))).astype(np.float32); shape = rng.integers(3, size=(N, 1, C))
    for k in ("x",):
        x = d[k].astype(np.float32)
        m = x.mean(axis=1, keepdims=True); level = m + np.sign(x - m) * np.abs(x - m).mean(axis=1, keepdims=True) * rng.uniform(0.9, 1.1, x.shape).astype(np.float32)
        other = x * np.where(rng.random(x.shape) < 0.016, 100.0, 1.0).astype(np.float32)
        d[k] = (np.where(shape == 1, level, np.where(shape == 2, other, x)) * f).astype(d[k].dtype)
    return d
def reference(x):
    X = x.astype(np.float64); U = X / np.sqrt((X ** 2).sum(axis=1, keepdims=True))
    y = np.full((N, C, N * C), np.nan)
    for r in range(N):
        for s in range(N):
            if s != r: y[r][:, C * s:C * s + C] = U[r].T @ U[s]
    return {"y": y.astype(ml_dtypes.bfloat16)}

@@ -1,0 +1,177 @@
+from concourse.bass import DstId, RemoteDMATransfer
+from concourse.mybir import AluOpType, ActivationFunctionType
+
+N = 8
+C = 128
+
+PLAN = (
+    (None, 0, 1, (4, 5), None),
+    (None, 0, 1, (1, 2, 3), None),
+    (0, 4, 2, (2,), None),
+)
+
+SCRATCH = {
+    "xs": ("sbuf", [128, N * C], "bfloat16"),
+    "sq": ("sbuf", [128, N * C], "bfloat16"),
+    "bt": ("sbuf", [128, N * C], "bfloat16"),
+    "ys": ("sbuf", [128, N * C], "bfloat16"),
+    "ones": ("sbuf", [128, C], "bfloat16"),
+    "ident": ("sbuf", [128, C], "bfloat16"),
+    "nrm": ("sbuf", [128, N], "float32"),
+    "d": ("sbuf", [128, N], "float32"),
+}
+for _k in range(N):
+    SCRATCH["ps%d" % _k] = ("psum", [128, 512], "float32")
+
+SEMAPHORES = ["ld", "one", "idn", "sent", "st"]
+SEMAPHORES += ["arr%d" % _c for _c in range(len(PLAN))]
+SEMAPHORES += ["%s%d" % (_n, _c) for _n in "nrd" for _c in range(len(PLAN) + 1)]
+SEMAPHORES += ["%s%d" % (_n, _k) for _n in "qabcy" for _k in range(N)]
+
+
+def rank_program(g, core, T, topo):
+    if T.rank_of(core) is None:
+        return
+    cores = list(T.cores)
+    V, S, P, Y = g.vector, g.scalar, g.tensor, g.sync
+    sem = T.sem
+
+    def pos(me, o):
+        if topo.host(o) == topo.host(me):
+            base = 0
+        elif topo.rack(topo.host(o)) == topo.rack(topo.host(me)):
+            base = 2
+        elif topo.may_write(me, o):
+            base = 4
+        else:
+            base = 6
+        return base + (0 if topo.chip(o) == topo.chip(me) else 1)
+
+    def table(me):
+        return dict((pos(me, o), o) for o in cores)
+
+    at = table(core)
+
+    def blk(t, k, n=1):
+        return t[:, k * C:(k + n) * C]
+
+    total, seen, done = {}, {}, set()
+
+    def inc(ins, name, n=1):
+        ins.then_inc(sem[name], n)
+        total[name] = total.get(name, 0) + n
+
+    def wait(q, qn, name, val):
+        if (qn, name, val) not in done:
+            done.add((qn, name, val))
+            q.wait_ge(sem[name], val)
+            seen[name] = max(seen.get(name, 0), val)
+
+    def engines(src, dests, part):
+        m = topo.mask(src, dests[0])
+        for o in dests[1:]:
+            m &= topo.mask(src, o)
+        if part is not None:
+            bits = [b for b in range(m.bit_length()) if (m >> b) & 1][part[0]:part[0] + part[1]]
+            m = sum(1 << b for b in bits)
+        return m
+
+    groups = []
+    for ci, (dep, lo, n, where, part) in enumerate(PLAN):
+        ks, cnt = [], 0
+        for p in where:
+            o = at[p]
+            to = table(o)
+            ks += [pos(core, to[lo + t]) for t in range(n)]
+            cnt += bin(engines(o, [to[w] for w in where], part)).count("1")
+        groups.append((ks, cnt))
+        total["arr%d" % ci] = cnt
+
+    inc(Y.dma_start(blk(T.xs, 0), T.x[:]), "ld", 16)
+    inc(V.memset(T.ones[:], 1.0), "one")
+    wait(g, "g", "one", 1)
+    inc(g.affine_select(T.ident[:], T.ones[:], [[-1, C]], AluOpType.is_equal, 0.0, 0, 1), "idn")
+
+    wait(g, "g", "ld", 16)
+    for ci, (dep, lo, n, where, part) in enumerate(PLAN):
+        if dep is not None:
+            wait(g, "g", "arr%d" % dep, groups[dep][1])
+        dests = [at[p] for p in where]
+        m = engines(core, dests, part)
+        ids, dsts = [], []
+        for o in dests:
+            l = pos(o, at[lo])
+            for t in range(n):
+                assert pos(o, at[lo + t]) == l + t
+            ids.append(topo.addr(o, core))
+            dsts.append(blk(T.xs, l, n))
+        if len(dests) == 1:
+            g.remote_dma(dsts[0], blk(T.xs, lo, n), sem["arr%d" % ci], sem["sent"], ids[0][1], ids[0][0], m)
+        else:
+            g.remote_dma_fused([RemoteDMATransfer(dst_ids=[DstId(rid=r, pnc=p) for r, p in ids], dma_engine_mask=m,
+                                                  remote_sem=sem["arr%d" % ci], srcs=[blk(T.xs, lo, n)], dsts=dsts,
+                                                  alu_op=0)], local_sem=sem["sent"])
+        total["sent"] = total.get("sent", 0) + bin(m).count("1")
+
+    one = T.ones[:, 0:1]
+    work = [([0], "ld", 16)] + [(ks, "arr%d" % ci, cnt) for ci, (ks, cnt) in enumerate(groups)]
+    col = 0
+    for gi, (ks, arr, cnt) in enumerate(work):
+        c0, c1 = col, col + len(ks)
+        col = c1
+        last = gi == len(work) - 1
+        wait(S, "s", arr, cnt)
+        for k in ks:
+            inc(S.activation(blk(T.sq, k), blk(T.xs, k), ActivationFunctionType.Square), "q%d" % k)
+        wait(P, "p", "ld", 16)
+        wait(P, "p", arr, cnt)
+        if gi:
+            for k in ks:
+                inc(P.matmul(T["ps%d" % k][:, 0:C], blk(T.xs, k), blk(T.xs, 0), True, True), "a%d" % k)
+            wait(P, "p", "r%d" % (gi - 1), 1)
+        wait(P, "p", "one", 1)
+        for j, k in enumerate(ks):
+            wait(P, "p", "q%d" % k, 1)
+            inc(P.matmul(T.ps0[:, c0 + j:c0 + j + 1], blk(T.sq, k), one, True, True), "n%d" % gi)
+        wait(S, "s", "n%d" % gi, len(ks))
+        inc(S.activation(T.nrm[:, c0:c1], T.ps0[:, c0:c1], ActivationFunctionType.Sqrt), "r%d" % gi)
+        wait(V, "v", "r%d" % gi, 1)
+        inc(V.reciprocal(T.d[:, c0:c1], T.nrm[:, c0:c1]), "d%d" % gi)
+        if not gi:
+            continue
+
+        def scaled(j, out, in_, column):
+            if j % 2 == 0:
+                return V.tensor_scalar(out, in_, column, None, AluOpType.mult)
+            return S.activation(out, in_, ActivationFunctionType.Identity, scale=column)
+
+        lane = [(V, "v") if j % 2 == 0 else (S, "s") for j in range(len(ks))]
+        for j, k in enumerate(ks):
+            wait(lane[j][0], lane[j][1], "d%d" % gi, 1)
+            wait(lane[j][0], lane[j][1], "a%d" % k, 1)
+            inc(scaled(j, blk(T.bt, k), T["ps%d" % k][:, 0:C], T.d[:, c0 + j:c0 + j + 1]), "b%d" % k)
+        wait(P, "p", "idn", 1)
+        for k in ks:
+            wait(P, "p", "b%d" % k, 1)
+            inc(P.matmul(T["ps%d" % k][:, C:2 * C], blk(T.bt, k), T.ident[:], True, True), "c%d" % k)
+        for j, k in enumerate(ks):
+            wait(lane[j][0], lane[j][1], "d0", 1)
+            wait(lane[j][0], lane[j][1], "c%d" % k, 1)
+            inc(scaled(j, blk(T.ys, T.rank_of(at[k])), T["ps%d" % k][:, C:2 * C], T.d[:, 0:1]), "y%d" % k)
+
+        byrank = sorted((T.rank_of(at[k]), j, k) for j, k in enumerate(ks))
+        runs = []
+        for s, j, k in byrank:
+            if runs and not last and runs[-1][-1][0] + 1 == s:
+                runs[-1].append((s, j, k))
+            else:
+                runs.append([(s, j, k)])
+        for run in runs:
+            q, qn = (S, "s") if last and all(j % 2 for s, j, k in run) else (Y, "y")
+            for s, j, k in run:
+                wait(q, qn, "y%d" % k, 1)
+            inc(q.dma_start(blk(T.y, run[0][0], len(run)), blk(T.ys, run[0][0], len(run))), "st", 16)
+
+    for name in sorted(total):
+        if seen.get(name, 0) < total[name]:
+            wait(g, "g", name, total[name])

@@ -5,9 +5,9 @@ N = 8
 C = 128
 
 PLAN = (
-    (None, 0, 1, (4, 5), None),
-    (None, 0, 1, (1, 2, 3), None),
-    (0, 4, 2, (2,), None),
+    (None, ((0, 1, (4,), (0, 4)), (0, 1, (3,), (4, 4)))),
+    (None, ((0, 1, (1, 2, 5), None),)),
+    (0, ((4, 1, (2,), (0, 4)), (3, 1, (4,), (4, 4)))),
 )
 
 SCRATCH = {
@@ -77,13 +77,14 @@ def rank_program(g, core, T, topo):
         return m
 
     groups = []
-    for ci, (dep, lo, n, where, part) in enumerate(PLAN):
+    for ci, (dep, transfers) in enumerate(PLAN):
         ks, cnt = [], 0
-        for p in where:
-            o = at[p]
-            to = table(o)
-            ks += [pos(core, to[lo + t]) for t in range(n)]
-            cnt += bin(engines(o, [to[w] for w in where], part)).count("1")
+        for lo, n, where, part in transfers:
+            for p in where:
+                o = at[p]
+                to = table(o)
+                ks += [pos(core, to[lo + t]) for t in range(n)]
+                cnt += bin(engines(o, [to[w] for w in where], part)).count("1")
         groups.append((ks, cnt))
         total["arr%d" % ci] = cnt
 
@@ -93,25 +94,25 @@ def rank_program(g, core, T, topo):
     inc(g.affine_select(T.ident[:], T.ones[:], [[-1, C]], AluOpType.is_equal, 0.0, 0, 1), "idn")
 
     wait(g, "g", "ld", 16)
-    for ci, (dep, lo, n, where, part) in enumerate(PLAN):
+    for ci, (dep, transfers) in enumerate(PLAN):
         if dep is not None:
             wait(g, "g", "arr%d" % dep, groups[dep][1])
-        dests = [at[p] for p in where]
-        m = engines(core, dests, part)
-        ids, dsts = [], []
-        for o in dests:
-            l = pos(o, at[lo])
-            for t in range(n):
-                assert pos(o, at[lo + t]) == l + t
-            ids.append(topo.addr(o, core))
-            dsts.append(blk(T.xs, l, n))
-        if len(dests) == 1:
-            g.remote_dma(dsts[0], blk(T.xs, lo, n), sem["arr%d" % ci], sem["sent"], ids[0][1], ids[0][0], m)
-        else:
-            g.remote_dma_fused([RemoteDMATransfer(dst_ids=[DstId(rid=r, pnc=p) for r, p in ids], dma_engine_mask=m,
-                                                  remote_sem=sem["arr%d" % ci], srcs=[blk(T.xs, lo, n)], dsts=dsts,
-                                                  alu_op=0)], local_sem=sem["sent"])
-        total["sent"] = total.get("sent", 0) + bin(m).count("1")
+        trs = []
+        for lo, n, where, part in transfers:
+            dests = [at[p] for p in where]
+            m = engines(core, dests, part)
+            ids, dsts = [], []
+            for o in dests:
+                l = pos(o, at[lo])
+                for t in range(n):
+                    assert pos(o, at[lo + t]) == l + t
+                r, p = topo.addr(o, core)
+                ids.append(DstId(rid=r, pnc=p))
+                dsts.append(blk(T.xs, l, n))
+            trs.append(RemoteDMATransfer(dst_ids=ids, dma_engine_mask=m, remote_sem=sem["arr%d" % ci],
+                                         srcs=[blk(T.xs, lo, n)], dsts=dsts, alu_op=0))
+            total["sent"] = total.get("sent", 0) + bin(m).count("1")
+        g.remote_dma_fused(trs, local_sem=sem["sent"])
 
     one = T.ones[:, 0:1]
     work = [([0], "ld", 16)] + [(ks, "arr%d" % ci, cnt) for ci, (ks, cnt) in enumerate(groups)]

@@ -34,6 +34,7 @@ def rank_program(g, core, T, topo):
         return
     cores = list(T.cores)
     V, S, P, Y = g.vector, g.scalar, g.tensor, g.sync
+    QN = {"v": V, "s": S, "p": P, "y": Y, "g": g}
     sem = T.sem
 
     def pos(me, o):
@@ -61,10 +62,10 @@ def rank_program(g, core, T, topo):
         ins.then_inc(sem[name], n)
         total[name] = total.get(name, 0) + n
 
-    def wait(q, qn, name, val):
+    def wait(qn, name, val):
         if (qn, name, val) not in done:
             done.add((qn, name, val))
-            q.wait_ge(sem[name], val)
+            QN[qn].wait_ge(sem[name], val)
             seen[name] = max(seen.get(name, 0), val)
 
     def engines(src, dests, part):
@@ -90,13 +91,13 @@ def rank_program(g, core, T, topo):
 
     inc(Y.dma_start(blk(T.xs, 0), T.x[:]), "ld", 16)
     inc(V.memset(T.ones[:], 1.0), "one")
-    wait(g, "g", "one", 1)
+    wait("g", "one", 1)
     inc(g.affine_select(T.ident[:], T.ones[:], [[-1, C]], AluOpType.is_equal, 0.0, 0, 1), "idn")
 
-    wait(g, "g", "ld", 16)
+    wait("g", "ld", 16)
     for ci, (dep, transfers) in enumerate(PLAN):
         if dep is not None:
-            wait(g, "g", "arr%d" % dep, groups[dep][1])
+            wait("g", "arr%d" % dep, groups[dep][1])
         trs = []
         for lo, n, where, part in transfers:
             dests = [at[p] for p in where]
@@ -114,65 +115,142 @@ def rank_program(g, core, T, topo):
             total["sent"] = total.get("sent", 0) + bin(m).count("1")
         g.remote_dma_fused(trs, local_sem=sem["sent"])
 
-    one = T.ones[:, 0:1]
     work = [([0], "ld", 16)] + [(ks, "arr%d" % ci, cnt) for ci, (ks, cnt) in enumerate(groups)]
-    col = 0
+    grp, dcol, span, col = {}, {}, [], 0
     for gi, (ks, arr, cnt) in enumerate(work):
-        c0, c1 = col, col + len(ks)
-        col = c1
-        last = gi == len(work) - 1
-        wait(S, "s", arr, cnt)
+        span.append((col, col + len(ks)))
         for k in ks:
+            grp[k], dcol[k] = gi, col
+            col += 1
+
+    def landed(qn, k):
+        wait(qn, work[grp[k]][1], work[grp[k]][2])
+
+    def square(qn, k):
+        landed(qn, k)
+        if qn == "s":
             inc(S.activation(blk(T.sq, k), blk(T.xs, k), ActivationFunctionType.Square), "q%d" % k)
-        wait(P, "p", "ld", 16)
-        wait(P, "p", arr, cnt)
+        else:
+            inc(V.tensor_tensor(blk(T.sq, k), blk(T.xs, k), blk(T.xs, k), AluOpType.mult), "q%d" % k)
+
+    def gram(k):
+        wait("p", "ld", 16)
+        landed("p", k)
+        inc(P.matmul(T["ps%d" % k][:, 0:C], blk(T.xs, k), blk(T.xs, 0), True, True), "a%d" % k)
+
+    def sums(k):
+        gi = grp[k]
+        wait("p", "one", 1)
         if gi:
-            for k in ks:
-                inc(P.matmul(T["ps%d" % k][:, 0:C], blk(T.xs, k), blk(T.xs, 0), True, True), "a%d" % k)
-            wait(P, "p", "r%d" % (gi - 1), 1)
-        wait(P, "p", "one", 1)
-        for j, k in enumerate(ks):
-            wait(P, "p", "q%d" % k, 1)
-            inc(P.matmul(T.ps0[:, c0 + j:c0 + j + 1], blk(T.sq, k), one, True, True), "n%d" % gi)
-        wait(S, "s", "n%d" % gi, len(ks))
+            wait("p", "r%d" % (gi - 1), 1)
+        wait("p", "q%d" % k, 1)
+        inc(P.matmul(T.ps0[:, dcol[k]:dcol[k] + 1], blk(T.sq, k), T.ones[:, 0:1], True, True), "n%d" % gi)
+
+    def root(gi):
+        c0, c1 = span[gi]
+        wait("s", "n%d" % gi, c1 - c0)
         inc(S.activation(T.nrm[:, c0:c1], T.ps0[:, c0:c1], ActivationFunctionType.Sqrt), "r%d" % gi)
-        wait(V, "v", "r%d" % gi, 1)
+
+    def recip(gi):
+        c0, c1 = span[gi]
+        wait("v", "r%d" % gi, 1)
         inc(V.reciprocal(T.d[:, c0:c1], T.nrm[:, c0:c1]), "d%d" % gi)
-        if not gi:
-            continue
 
-        def scaled(j, out, in_, column):
-            if j % 2 == 0:
-                return V.tensor_scalar(out, in_, column, None, AluOpType.mult)
-            return S.activation(out, in_, ActivationFunctionType.Identity, scale=column)
+    def scaled(qn, out, in_, column):
+        if qn == "v":
+            return V.tensor_scalar(out, in_, column, None, AluOpType.mult)
+        return S.activation(out, in_, ActivationFunctionType.Identity, scale=column)
 
-        lane = [(V, "v") if j % 2 == 0 else (S, "s") for j in range(len(ks))]
-        for j, k in enumerate(ks):
-            wait(lane[j][0], lane[j][1], "d%d" % gi, 1)
-            wait(lane[j][0], lane[j][1], "a%d" % k, 1)
-            inc(scaled(j, blk(T.bt, k), T["ps%d" % k][:, 0:C], T.d[:, c0 + j:c0 + j + 1]), "b%d" % k)
-        wait(P, "p", "idn", 1)
+    def first(qn, k):
+        wait(qn, "d%d" % grp[k], 1)
+        wait(qn, "a%d" % k, 1)
+        inc(scaled(qn, blk(T.bt, k), T["ps%d" % k][:, 0:C], T.d[:, dcol[k]:dcol[k] + 1]), "b%d" % k)
+
+    def turn(k):
+        wait("p", "idn", 1)
+        wait("p", "b%d" % k, 1)
+        inc(P.matmul(T["ps%d" % k][:, C:2 * C], blk(T.bt, k), T.ident[:], True, True), "c%d" % k)
+
+    def second(qn, k):
+        wait(qn, "d0", 1)
+        wait(qn, "c%d" % k, 1)
+        inc(scaled(qn, blk(T.ys, T.rank_of(at[k])), T["ps%d" % k][:, C:2 * C], T.d[:, 0:1]), "y%d" % k)
+
+    def store(qn, ks):
+        rs = sorted(T.rank_of(at[k]) for k in ks)
+        assert rs == list(range(rs[0], rs[0] + len(rs)))
         for k in ks:
-            wait(P, "p", "b%d" % k, 1)
-            inc(P.matmul(T["ps%d" % k][:, C:2 * C], blk(T.bt, k), T.ident[:], True, True), "c%d" % k)
-        for j, k in enumerate(ks):
-            wait(lane[j][0], lane[j][1], "d0", 1)
-            wait(lane[j][0], lane[j][1], "c%d" % k, 1)
-            inc(scaled(j, blk(T.ys, T.rank_of(at[k])), T["ps%d" % k][:, C:2 * C], T.d[:, 0:1]), "y%d" % k)
+            wait(qn, "y%d" % k, 1)
+        inc(QN[qn].dma_start(blk(T.y, rs[0], len(rs)), blk(T.ys, rs[0], len(rs))), "st", 16)
 
-        byrank = sorted((T.rank_of(at[k]), j, k) for j, k in enumerate(ks))
-        runs = []
-        for s, j, k in byrank:
-            if runs and not last and runs[-1][-1][0] + 1 == s:
-                runs[-1].append((s, j, k))
-            else:
-                runs.append([(s, j, k)])
-        for run in runs:
-            q, qn = (S, "s") if last and all(j % 2 for s, j, k in run) else (Y, "y")
-            for s, j, k in run:
-                wait(q, qn, "y%d" % k, 1)
-            inc(q.dma_start(blk(T.y, run[0][0], len(run)), blk(T.ys, run[0][0], len(run))), "st", 16)
+    (k1, k2), (a, b, c), (e, f) = work[1][0], work[2][0], work[3][0]
+
+    square("s", 0)
+    root(0)
+    square("s", k1)
+    square("s", k2)
+    root(1)
+    first("s", k2)
+    second("s", k2)
+    square("s", a)
+    square("s", b)
+    root(2)
+    square("s", e)
+    square("s", f)
+    root(3)
+    first("s", b)
+    first("s", f)
+    second("s", b)
+    second("s", f)
+    store("s", [f])
+
+    recip(0)
+    recip(1)
+    first("v", k1)
+    second("v", k1)
+    square("v", c)
+    recip(2)
+    first("v", a)
+    first("v", c)
+    recip(3)
+    first("v", e)
+    second("v", a)
+    second("v", c)
+    second("v", e)
+
+    sums(0)
+    gram(k1)
+    sums(k1)
+    sums(k2)
+    gram(k2)
+    turn(k1)
+    turn(k2)
+    gram(a)
+    sums(a)
+    sums(b)
+    sums(c)
+    gram(b)
+    gram(c)
+    sums(e)
+    sums(f)
+    gram(e)
+    gram(f)
+    turn(a)
+    turn(c)
+    turn(b)
+    turn(e)
+    turn(f)
+
+    if abs(T.rank_of(at[k1]) - T.rank_of(at[k2])) == 1:
+        store("y", [k1, k2])
+    else:
+        store("y", [k1])
+        store("y", [k2])
+    store("y", [a])
+    store("y", [c])
+    store("y", [b])
+    store("y", [e])
 
     for name in sorted(total):
         if seen.get(name, 0) < total[name]:
-            wait(g, "g", name, total[name])
+            wait("g", name, total[name])

from concourse.bass import DstId, RemoteDMATransfer
from concourse.mybir import AluOpType, ActivationFunctionType

N = 8
C = 128

PLAN = (
    (None, ((0, 1, (4,), (0, 4)), (0, 1, (3,), (4, 4)))),
    (None, ((0, 1, (1, 2, 5), None),)),
    (0, ((4, 1, (2,), (0, 4)), (3, 1, (4,), (4, 4)))),
)

SCRATCH = {
    "xs": ("sbuf", [128, N * C], "bfloat16"),
    "sq": ("sbuf", [128, N * C], "bfloat16"),
    "bt": ("sbuf", [128, N * C], "bfloat16"),
    "ys": ("sbuf", [128, N * C], "bfloat16"),
    "ones": ("sbuf", [128, C], "bfloat16"),
    "ident": ("sbuf", [128, C], "bfloat16"),
    "nrm": ("sbuf", [128, N], "float32"),
    "d": ("sbuf", [128, N], "float32"),
}
for _k in range(N):
    SCRATCH["ps%d" % _k] = ("psum", [128, 512], "float32")

SEMAPHORES = ["ld", "one", "idn", "sent", "st"]
SEMAPHORES += ["arr%d" % _c for _c in range(len(PLAN))]
SEMAPHORES += ["%s%d" % (_n, _c) for _n in "nrd" for _c in range(len(PLAN) + 1)]
SEMAPHORES += ["%s%d" % (_n, _k) for _n in "qabcy" for _k in range(N)]


def rank_program(g, core, T, topo):
    if T.rank_of(core) is None:
        return
    cores = list(T.cores)
    V, S, P, Y = g.vector, g.scalar, g.tensor, g.sync
    QN = {"v": V, "s": S, "p": P, "y": Y, "g": g}
    sem = T.sem

    def pos(me, o):
        if topo.host(o) == topo.host(me):
            base = 0
        elif topo.rack(topo.host(o)) == topo.rack(topo.host(me)):
            base = 2
        elif topo.may_write(me, o):
            base = 4
        else:
            base = 6
        return base + (0 if topo.chip(o) == topo.chip(me) else 1)

    def table(me):
        return dict((pos(me, o), o) for o in cores)

    at = table(core)

    def blk(t, k, n=1):
        return t[:, k * C:(k + n) * C]

    total, seen, done = {}, {}, set()

    def inc(ins, name, n=1):
        ins.then_inc(sem[name], n)
        total[name] = total.get(name, 0) + n

    def wait(qn, name, val):
        if (qn, name, val) not in done:
            done.add((qn, name, val))
            QN[qn].wait_ge(sem[name], val)
            seen[name] = max(seen.get(name, 0), val)

    def engines(src, dests, part):
        m = topo.mask(src, dests[0])
        for o in dests[1:]:
            m &= topo.mask(src, o)
        if part is not None:
            bits = [b for b in range(m.bit_length()) if (m >> b) & 1][part[0]:part[0] + part[1]]
            m = sum(1 << b for b in bits)
        return m

    groups = []
    for ci, (dep, transfers) in enumerate(PLAN):
        ks, cnt = [], 0
        for lo, n, where, part in transfers:
            for p in where:
                o = at[p]
                to = table(o)
                ks += [pos(core, to[lo + t]) for t in range(n)]
                cnt += bin(engines(o, [to[w] for w in where], part)).count("1")
        groups.append((ks, cnt))
        total["arr%d" % ci] = cnt

    inc(Y.dma_start(blk(T.xs, 0), T.x[:]), "ld", 16)
    inc(V.memset(T.ones[:], 1.0), "one")
    wait("g", "one", 1)
    inc(g.affine_select(T.ident[:], T.ones[:], [[-1, C]], AluOpType.is_equal, 0.0, 0, 1), "idn")

    wait("g", "ld", 16)
    for ci, (dep, transfers) in enumerate(PLAN):
        if dep is not None:
            wait("g", "arr%d" % dep, groups[dep][1])
        trs = []
        for lo, n, where, part in transfers:
            dests = [at[p] for p in where]
            m = engines(core, dests, part)
            ids, dsts = [], []
            for o in dests:
                l = pos(o, at[lo])
                for t in range(n):
                    assert pos(o, at[lo + t]) == l + t
                r, p = topo.addr(o, core)
                ids.append(DstId(rid=r, pnc=p))
                dsts.append(blk(T.xs, l, n))
            trs.append(RemoteDMATransfer(dst_ids=ids, dma_engine_mask=m, remote_sem=sem["arr%d" % ci],
                                         srcs=[blk(T.xs, lo, n)], dsts=dsts, alu_op=0))
            total["sent"] = total.get("sent", 0) + bin(m).count("1")
        g.remote_dma_fused(trs, local_sem=sem["sent"])

    work = [([0], "ld", 16)] + [(ks, "arr%d" % ci, cnt) for ci, (ks, cnt) in enumerate(groups)]
    grp, dcol, span, col = {}, {}, [], 0
    for gi, (ks, arr, cnt) in enumerate(work):
        span.append((col, col + len(ks)))
        for k in ks:
            grp[k], dcol[k] = gi, col
            col += 1

    def landed(qn, k):
        wait(qn, work[grp[k]][1], work[grp[k]][2])

    def square(qn, k):
        landed(qn, k)
        if qn == "s":
            inc(S.activation(blk(T.sq, k), blk(T.xs, k), ActivationFunctionType.Square), "q%d" % k)
        else:
            inc(V.tensor_tensor(blk(T.sq, k), blk(T.xs, k), blk(T.xs, k), AluOpType.mult), "q%d" % k)

    def gram(k):
        wait("p", "ld", 16)
        landed("p", k)
        inc(P.matmul(T["ps%d" % k][:, 0:C], blk(T.xs, k), blk(T.xs, 0), True, True), "a%d" % k)

    def sums(k):
        gi = grp[k]
        wait("p", "one", 1)
        if gi:
            wait("p", "r%d" % (gi - 1), 1)
        wait("p", "q%d" % k, 1)
        inc(P.matmul(T.ps0[:, dcol[k]:dcol[k] + 1], blk(T.sq, k), T.ones[:, 0:1], True, True), "n%d" % gi)

    def root(gi):
        c0, c1 = span[gi]
        wait("s", "n%d" % gi, c1 - c0)
        inc(S.activation(T.nrm[:, c0:c1], T.ps0[:, c0:c1], ActivationFunctionType.Sqrt), "r%d" % gi)

    def recip(gi):
        c0, c1 = span[gi]
        wait("v", "r%d" % gi, 1)
        inc(V.reciprocal(T.d[:, c0:c1], T.nrm[:, c0:c1]), "d%d" % gi)

    def scaled(qn, out, in_, column):
        if qn == "v":
            return V.tensor_scalar(out, in_, column, None, AluOpType.mult)
        return S.activation(out, in_, ActivationFunctionType.Identity, scale=column)

    def first(qn, k):
        wait(qn, "d%d" % grp[k], 1)
        wait(qn, "a%d" % k, 1)
        inc(scaled(qn, blk(T.bt, k), T["ps%d" % k][:, 0:C], T.d[:, dcol[k]:dcol[k] + 1]), "b%d" % k)

    def turn(k):
        wait("p", "idn", 1)
        wait("p", "b%d" % k, 1)
        inc(P.matmul(T["ps%d" % k][:, C:2 * C], blk(T.bt, k), T.ident[:], True, True), "c%d" % k)

    def second(qn, k):
        wait(qn, "d0", 1)
        wait(qn, "c%d" % k, 1)
        inc(scaled(qn, blk(T.ys, T.rank_of(at[k])), T["ps%d" % k][:, C:2 * C], T.d[:, 0:1]), "y%d" % k)

    def store(qn, ks):
        rs = sorted(T.rank_of(at[k]) for k in ks)
        assert rs == list(range(rs[0], rs[0] + len(rs)))
        for k in ks:
            wait(qn, "y%d" % k, 1)
        inc(QN[qn].dma_start(blk(T.y, rs[0], len(rs)), blk(T.ys, rs[0], len(rs))), "st", 16)

    (k1, k2), (a, b, c), (e, f) = work[1][0], work[2][0], work[3][0]

    square("s", 0)
    root(0)
    square("s", k1)
    square("s", k2)
    root(1)
    first("s", k2)
    second("s", k2)
    square("s", a)
    square("s", b)
    root(2)
    square("s", e)
    square("s", f)
    root(3)
    first("s", b)
    first("s", f)
    second("s", b)
    second("s", f)
    store("s", [f])

    recip(0)
    recip(1)
    first("v", k1)
    second("v", k1)
    square("v", c)
    recip(2)
    first("v", a)
    first("v", c)
    recip(3)
    first("v", e)
    second("v", a)
    second("v", c)
    second("v", e)

    sums(0)
    gram(k1)
    sums(k1)
    sums(k2)
    gram(k2)
    turn(k1)
    turn(k2)
    gram(a)
    sums(a)
    sums(b)
    sums(c)
    gram(b)
    gram(c)
    sums(e)
    sums(f)
    gram(e)
    gram(f)
    turn(a)
    turn(c)
    turn(b)
    turn(e)
    turn(f)

    if abs(T.rank_of(at[k1]) - T.rank_of(at[k2])) == 1:
        store("y", [k1, k2])
    else:
        store("y", [k1])
        store("y", [k2])
    store("y", [a])
    store("y", [c])
    store("y", [b])
    store("y", [e])

    for name in sorted(total):
        if seen.get(name, 0) < total[name]:
            wait("g", name, total[name])
